import numpy as np, ml_dtypes
CORES = [64,68,72,76,80,84,88,92,96,100,104,108,112,116,120,124]
N = 16
GROUPS = [[0,1],[2,3],[4,5],[6,7],[8,9],[10,11],[12,13],[14,15]]
def setup_inputs(rng):
    return {"x": rng.standard_normal((N, 128, 2048), dtype=np.float32).astype(ml_dtypes.bfloat16)}
def reference(x):
    y = np.empty((N, 128, 4096), x.dtype)
    for g in GROUPS:
        s = np.concatenate([x[r] for r in g], axis=1)
        for r in g:
            y[r] = s
    return {"y": y}

W = 2048
NCH = 2
CW = W // NCH

SCRATCH = {
    "stage": ("sbuf", [128, W], "bfloat16"),
    "land": ("sbuf", [128, W], "bfloat16"),
}
SEMAPHORES = ["ld%d" % k for k in range(NCH)] + ["ar%d" % k for k in range(NCH)] + ["sent", "stored"]


def rank_program(g, core, T, topo):
    rank = T.rank_of(core)
    if rank is None:
        return

    group = [grp for grp in T.tables["GROUPS"] if rank in grp][0]
    pos = group.index(rank)
    ppos = 1 - pos
    peer = T.cores[group[ppos]]
    rid, pid, _se = topo.addr(peer)
    mask = topo.mask(core, peer)
    eng = bin(mask).count("1")

    for k in range(NCH):
        c = slice(k * CW, (k + 1) * CW)
        g.sync.dma_start(T.stage[:, c], T.x[:, c]).then_inc(T.sem["ld%d" % k], 16)

    g.scalar.dma_start(T.y[:, pos * W:(pos + 1) * W], T.x[:, :]).then_inc(T.sem.stored, 16)

    for k in range(NCH):
        c = slice(k * CW, (k + 1) * CW)
        g.wait_ge(T.sem["ld%d" % k], 16)
        g.remote_dma(T.land[:, c], T.stage[:, c], T.sem["ar%d" % k], T.sem.sent, pid, rid, mask)

    for k in range(NCH):
        q = g.sync if k % 2 == 0 else g.scalar
        q.wait_ge(T.sem["ar%d" % k], eng)
        q.dma_start(T.y[:, ppos * W + k * CW: ppos * W + (k + 1) * CW],
                    T.land[:, k * CW:(k + 1) * CW]).then_inc(T.sem.stored, 16)

    g.wait_ge(T.sem.sent, NCH * eng)
    g.wait_ge(T.sem.stored, 16 * (NCH + 1))
